import numpy as np, ml_dtypes
CORES = [12,28,44,60,3,19,35,51]
N = 8
import mx_ref
NC, KT = 512, 1
BF = ml_dtypes.bfloat16
def setup_inputs(rng):
    def f(*shape):
        return mx_ref.flush((rng.standard_normal(shape, dtype=np.float32) * np.exp2(rng.integers(-2, 3, shape[:-1] + (1,)))).astype(BF))
    return {"w": f(N, 128, KT * 512), "x": f(N, 128, KT * 4 * NC)}
def setup_inputs_blocks(rng):
    d = setup_inputs(rng)
    for k in ("w", "x"): d[k] = mx_ref.spread(d[k], rng, 4)
    return d
def setup_inputs_wide(rng):
    d = setup_inputs(rng)
    for k in ("w", "x"): d[k] = mx_ref.flush((d[k].astype(np.float32) * np.exp2(rng.integers(-8, 9, (N, 1, 1))).astype(np.float32)).astype(BF))
    return d
def setup_inputs_zeros(rng):
    d = setup_inputs(rng); v = d["x"].reshape(N, 128, -1, 4).copy()
    v[np.broadcast_to((rng.random((N, 1, v.shape[2], 1)) < 0.33), v.shape)] = 0
    d["x"] = v.reshape(d["x"].shape)
    return d
def reference(w, x):
    QW = [[mx_ref.quantize(w[r][:, 512 * t:512 * t + 512]) for t in range(KT)] for r in range(N)]
    QX = [[mx_ref.quantize(x[j][:, 4 * NC * t:4 * NC * t + 4 * NC]) for t in range(KT)] for j in range(N)]
    y = np.zeros((N, 128, N * NC), np.float32)
    for r in range(N):
        for j in range(N):
            for t in range(KT):
                p = mx_ref.matmul(QW[r][t], QX[j][t])
                y[r][:, NC * j:NC * j + NC] = p if t == 0 else y[r][:, NC * j:NC * j + NC] + p
    return {"y": y}

@@ -1,0 +1,181 @@
+from concourse.bass import DstId, RemoteDMATransfer
+from concourse.mybir import dt, ActivationFunctionType
+
+N = 8
+NC = 512
+NSIM = 64
+CUT = [0, 192, 384, 512]
+NP = len(CUT) - 1
+
+SCRATCH = {
+    "xb": ("sbuf", [128, 4 * NC], "bfloat16"),
+    "wb": ("sbuf", [128, 512], "bfloat16"),
+    "wc": ("sbuf", [128, 128], "float8_e4m3fn_x4"),
+    "ws": ("sbuf", [128, 128], "uint8"),
+    "xc": ("sbuf", [128, N * NC], "float8_e4m3fn_x4"),
+    "xs": ("sbuf", [128, N * NC], "uint8"),
+    "yb": ("sbuf", [128, N * NC], "float32"),
+    "ps": ("psum", [128, N * NC], "float32"),
+}
+SEMAPHORES = (["lw", "qw", "got", "sent", "sts", "sta", "mmx", "evx"]
+              + ["lx%d" % k for k in range(NP)] + ["q%d" % k for k in range(NP)]
+              + ["arr%d" % j for j in range(N)] + ["mm%d" % j for j in range(N)] + ["ev%d" % j for j in range(N)])
+
+
+def _engines(mask):
+    return sum((mask >> e) & 1 for e in range(16))
+
+
+def _share(mask, k, i):
+    bits = [e for e in range(16) if (mask >> e) & 1]
+    n = len(bits) // k
+    return sum(1 << e for e in bits[i * n:(i + 1) * n])
+
+
+def _plan(T, topo, j):
+    cores = list(T.cores)
+    R = cores[j]
+    ch = topo.chip(R)
+    plane = [c for c in cores if c == R or topo.same_plane(ch, topo.chip(c))]
+    other = [c for c in cores if c not in plane]
+    i = plane.index(R)
+    m = [k for k, c in enumerate(other) if topo.mates(ch, topo.chip(c))][0]
+    near = [plane[(i + s) % len(plane)] for s in range(1, len(plane))]
+    far = [other[(m + s) % len(other)] for s in range(1, len(other) + 1)]
+    mine = [c for c in range(NSIM) if topo.chip(c) == ch]
+    fx = [c for c in mine if all(topo.may_write(c, d) for d in far)]
+    nx = [c for c in mine if c not in fx]
+    jobs = {}
+    who = [[] for _ in range(NP + 1)]
+    for grp, dests in ((fx, far), (nx, near)):
+        away = [c for c in grp if c != R and topo.die(c) != topo.die(R)]
+        home = [c for c in grp if c != R and topo.die(c) == topo.die(R)]
+        if R in grp:
+            order = away[:1] + home + away[1:] + [R]
+        else:
+            order = away[1:] + home + away[:1]
+        for p, c in enumerate(order):
+            jobs[c] = (p, dests)
+            if c != R:
+                who[p].append(c)
+    calls = [[(p, who[p], 1, 0)] for p in range(NP - 1)]
+    calls.append([(NP - 1, who[NP - 1], 2, 0), (NP, who[NP], 2, 1)])
+    return calls, jobs, near, far
+
+
+def _view(T, j, p):
+    if p < NP:
+        return T.xc[:, NC * j + CUT[p]:NC * j + CUT[p + 1]].bitcast(dt.uint8)
+    return T.xs[:, NC * j:NC * j + NC]
+
+
+def _send(g, T, topo, src, j, items, rsem, lsem):
+    trs = []
+    used = 0
+    for p, dests, k, i in items:
+        mask = topo.mask(src, dests[0])
+        for d in dests:
+            mask &= topo.mask(src, d)
+        mask = _share(mask, k, i)
+        used += _engines(mask)
+        ids = [DstId(rid=topo.addr(d)[0], pnc=topo.addr(d)[1]) for d in dests]
+        trs.append(RemoteDMATransfer(dst_ids=ids, dma_engine_mask=mask, remote_sem=rsem,
+                                     srcs=[_view(T, j, p)], dsts=[_view(T, j, p) for _ in dests]))
+    g.remote_dma_fused(trs, local_sem=lsem)
+    return used
+
+
+def rank_program(g, core, T, topo):
+    S = T.sem
+    cores = list(T.cores)
+    rank = T.rank_of(core)
+    plans = [_plan(T, topo, j) for j in range(N)]
+
+    if rank is None:
+        for j in range(N):
+            calls, jobs, near, far = plans[j]
+            if core not in jobs:
+                continue
+            p, dests = jobs[core]
+            got = sum(_engines(_share(topo.mask(cores[j], core), k, i))
+                      for call in calls for (_, hs, k, i) in call if core in hs)
+            g.wait_ge(S.got, got)
+            sent = 0
+            for d in dests:
+                sent += _send(g, T, topo, core, j, [(p, [d], 1, 0)], S["arr%d" % j], S.sent)
+            g.wait_ge(S.sent, sent)
+        return
+
+    o = NC * rank
+    calls, jobs, near, far = plans[rank]
+
+    for k in range(NP):
+        q = g.sync if k % 2 == 0 else g.scalar
+        q.dma_start(T.xb[:, 4 * CUT[k]:4 * CUT[k + 1]], T.x[:, 4 * CUT[k]:4 * CUT[k + 1]]).then_inc(S["lx%d" % k], 16)
+    g.scalar.dma_start(T.wb[:], T.w[:]).then_inc(S.lw, 16)
+
+    for k in range(NP):
+        g.vector.wait_ge(S["lx%d" % k], 16)
+        g.vector.quantize_mx(T.xc[:, o + CUT[k]:o + CUT[k + 1]], T.xs[:, o + CUT[k]:o + CUT[k + 1]],
+                             T.xb[:, 4 * CUT[k]:4 * CUT[k + 1]]).then_inc(S["q%d" % k], 1)
+    g.vector.wait_ge(S.lw, 16)
+    g.vector.quantize_mx(T.wc[:], T.ws[:], T.wb[:]).then_inc(S.qw, 1)
+
+    sent = 0
+    for call in calls:
+        for p, _, _, _ in call:
+            if p < NP:
+                g.wait_ge(S["q%d" % p], 1)
+        sent += _send(g, T, topo, core, rank, call, S.got, S.sent)
+    p, dests = jobs[core]
+    sent += _send(g, T, topo, core, rank, [(p, dests, 1, 0)], S["arr%d" % rank], S.sent)
+
+    def slot(j):
+        _, _, nr, fr = plans[j]
+        return (nr.index(core), 0) if core in nr else (fr.index(core), 1)
+
+    def expect(j):
+        _, jb, _, _ = plans[j]
+        return sum(_engines(topo.mask(c, core)) for c, (p_, ds) in jb.items() if core in ds)
+
+    order = [rank] + sorted([j for j in range(N) if j != rank], key=slot)
+    g.tensor.wait_ge(S.qw, 1)
+    for k in range(NP):
+        g.tensor.wait_ge(S["q%d" % k], 1)
+    n_sync = n_act = 0
+    for i, j in enumerate(order[:-1]):
+        a, b = NC * j, NC * j + NC
+        if j != rank:
+            g.tensor.wait_ge(S["arr%d" % j], expect(j))
+        g.tensor.matmul_mx(T.ps[:, a:b], T.wc[:], T.ws[:], T.xc[:, a:b], T.xs[:, a:b], True, True).then_inc(S["mm%d" % j], 1)
+        if i % 2 == 0:
+            g.vector.wait_ge(S["mm%d" % j], 1)
+            g.vector.tensor_copy(T.yb[:, a:b], T.ps[:, a:b]).then_inc(S["ev%d" % j], 1)
+            g.sync.wait_ge(S["ev%d" % j], 1)
+            g.sync.dma_start(T.y[:, a:b], T.yb[:, a:b]).then_inc(S.sts, 16)
+            n_sync += 1
+        else:
+            g.scalar.wait_ge(S["mm%d" % j], 1)
+            g.scalar.activation(T.yb[:, a:b], T.ps[:, a:b], ActivationFunctionType.Copy).then_inc(S["ev%d" % j], 1)
+            g.scalar.wait_ge(S["ev%d" % j], 1)
+            g.scalar.dma_start(T.y[:, a:b], T.yb[:, a:b]).then_inc(S.sta, 16)
+            n_act += 1
+
+    j = order[-1]
+    a, h, b = NC * j, NC * j + NC // 2, NC * j + NC
+    g.tensor.wait_ge(S["arr%d" % j], expect(j))
+    g.tensor.matmul_mx(T.ps[:, a:h], T.wc[:], T.ws[:], T.xc[:, a:h], T.xs[:, a:h], True, True).then_inc(S["mm%d" % j], 1)
+    g.tensor.wait_ge(S["ev%d" % rank], 1)
+    g.tensor.matmul_mx(T.ps[:, o:o + NC // 2], T.wc[:], T.ws[:], T.xc[:, h:b], T.xs[:, h:b], True, True).then_inc(S.mmx, 1)
+    g.vector.wait_ge(S["mm%d" % j], 1)
+    g.vector.tensor_copy(T.yb[:, a:h], T.ps[:, a:h]).then_inc(S["ev%d" % j], 1)
+    g.sync.wait_ge(S["ev%d" % j], 1)
+    g.sync.dma_start(T.y[:, a:h], T.yb[:, a:h]).then_inc(S.sts, 16)
+    g.scalar.wait_ge(S.mmx, 1)
+    g.scalar.activation(T.yb[:, h:b], T.ps[:, o:o + NC // 2], ActivationFunctionType.Copy).then_inc(S.evx, 1)
+    g.scalar.wait_ge(S.evx, 1)
+    g.scalar.dma_start(T.y[:, h:b], T.yb[:, h:b]).then_inc(S.sta, 16)
+
+    g.sync.wait_ge(S.sts, 16 * (n_sync + 1))
+    g.scalar.wait_ge(S.sta, 16 * (n_act + 1))
+    g.wait_ge(S.sent, sent)

@@ -17,9 +17,10 @@ SCRATCH = {
     "yb": ("sbuf", [128, N * NC], "float32"),
     "ps": ("psum", [128, N * NC], "float32"),
 }
-SEMAPHORES = (["lw", "qw", "got", "sent", "sts", "sta", "mmx", "evx"]
+SEMAPHORES = (["lw", "qw", "sent", "sts", "sta", "mmx", "evx"]
               + ["lx%d" % k for k in range(NP)] + ["q%d" % k for k in range(NP)]
-              + ["arr%d" % j for j in range(N)] + ["mm%d" % j for j in range(N)] + ["ev%d" % j for j in range(N)])
+              + ["arr%d" % j for j in range(N)] + ["rel%d" % j for j in range(N)]
+              + ["mm%d" % j for j in range(N)] + ["ev%d" % j for j in range(N)])
 
 
 def _engines(mask):
@@ -32,35 +33,76 @@ def _share(mask, k, i):
     return sum(1 << e for e in bits[i * n:(i + 1) * n])
 
 
-def _plan(T, topo, j):
+def _plan(T, topo):
     cores = list(T.cores)
-    R = cores[j]
-    ch = topo.chip(R)
-    plane = [c for c in cores if c == R or topo.same_plane(ch, topo.chip(c))]
-    other = [c for c in cores if c not in plane]
-    i = plane.index(R)
-    m = [k for k, c in enumerate(other) if topo.mates(ch, topo.chip(c))][0]
-    near = [plane[(i + s) % len(plane)] for s in range(1, len(plane))]
-    far = [other[(m + s) % len(other)] for s in range(1, len(other) + 1)]
-    mine = [c for c in range(NSIM) if topo.chip(c) == ch]
-    fx = [c for c in mine if all(topo.may_write(c, d) for d in far)]
-    nx = [c for c in mine if c not in fx]
+    near, mate, PS, MS = [], [], [], []
+    for j, R in enumerate(cores):
+        ch = topo.chip(R)
+        plane = [k for k, c in enumerate(cores) if c == R or topo.same_plane(ch, topo.chip(c))]
+        i = plane.index(j)
+        near.append([plane[(i + s) % len(plane)] for s in range(1, len(plane))])
+        mate.append([k for k, c in enumerate(cores) if topo.mates(ch, topo.chip(c))][0])
+    for j, R in enumerate(cores):
+        mine = [c for c in range(NSIM) if topo.chip(c) == topo.chip(R)]
+        own = [c for c in mine if topo.may_write(c, cores[mate[j]])]
+        rest = [c for c in mine if c not in own]
+        for grp, out in ((own, MS), (rest, PS)):
+            away = [c for c in grp if c != R and topo.die(c) != topo.die(R)]
+            home = [c for c in grp if c != R and topo.die(c) == topo.die(R)]
+            if R in grp:
+                out.append(away[:1] + home + away[1:] + [R])
+            else:
+                out.append(away[1:] + home + away[:1])
+
     jobs = {}
-    who = [[] for _ in range(NP + 1)]
-    for grp, dests in ((fx, far), (nx, near)):
-        away = [c for c in grp if c != R and topo.die(c) != topo.die(R)]
-        home = [c for c in grp if c != R and topo.die(c) == topo.die(R)]
-        if R in grp:
-            order = away[:1] + home + away[1:] + [R]
-        else:
-            order = away[1:] + home + away[:1]
-        for p, c in enumerate(order):
-            jobs[c] = (p, dests)
-            if c != R:
-                who[p].append(c)
-    calls = [[(p, who[p], 1, 0)] for p in range(NP - 1)]
-    calls.append([(NP - 1, who[NP - 1], 2, 0), (NP, who[NP], 2, 1)])
-    return calls, jobs, near, far
+    when = {}
+
+    def job(core, turn, j, p, calls):
+        jobs.setdefault(core, []).append((turn, j, p, calls))
+
+    def one(src, p, d):
+        return [(p, [d], topo.mask(src, d))]
+
+    for j, R in enumerate(cores):
+        c1, c2, c3 = near[j]
+        who = [[c for c in (PS[j][p], MS[j][p]) if c != R] for p in range(NP + 1)]
+        full = topo.mask(R, who[0][0])
+        hand = [[(p, who[p], full)] for p in range(NP - 1)]
+        hand.append([(NP - 1, who[NP - 1], _share(full, 2, 0)), (NP, who[NP], _share(full, 2, 1))])
+        job(R, -1, j, None, hand)
+        for p in range(NP + 1):
+            a, b = PS[j][p], MS[j][p]
+            job(a, 0, j, p, [one(a, p, MS[c1][p]), one(a, p, MS[c2][p]), one(a, p, cores[c3])])
+            job(b, 0, j, p, [one(b, p, cores[mate[c3]]), one(b, p, cores[mate[j]])])
+            for turn, c in ((1, c1), (2, c2)):
+                q = MS[c][p]
+                off = topo.mask(q, cores[mate[c]])
+                call = [(p, [cores[mate[c]]], off)]
+                if q != cores[c]:
+                    call.insert(0, (p, [cores[c]], topo.mask(q, cores[c]) & ~off))
+                job(q, turn, j, p, [call])
+        when[(cores[mate[c3]], j)] = (0, 0)
+        when[(cores[mate[j]], j)] = (0, 1)
+        when[(cores[c3], j)] = (0, 2)
+        for turn, c in ((1, c1), (2, c2)):
+            when[(cores[c], j)] = (turn, 0)
+            when[(cores[mate[c]], j)] = (turn, 1)
+
+    passes = set((core, j, p) for core, js in jobs.items() for (_, j, p, _) in js if p is not None)
+
+    def sem(d, j, p):
+        return ("rel%d" if (d in cores and (d, j, p) in passes) else "arr%d") % j
+
+    land = {}
+    for core, js in jobs.items():
+        js.sort(key=lambda t: t[0])
+        for (_, j, _, calls) in js:
+            for call in calls:
+                for (p, dests, mask) in call:
+                    for d in dests:
+                        k = (d, sem(d, j, p))
+                        land[k] = land.get(k, 0) + _engines(mask)
+    return jobs, land, when, sem
 
 
 def _view(T, j, p):
@@ -69,19 +111,15 @@ def _view(T, j, p):
     return T.xs[:, NC * j:NC * j + NC]
 
 
-def _send(g, T, topo, src, j, items, rsem, lsem):
+def _send(g, T, topo, j, call, sem):
     trs = []
     used = 0
-    for p, dests, k, i in items:
-        mask = topo.mask(src, dests[0])
-        for d in dests:
-            mask &= topo.mask(src, d)
-        mask = _share(mask, k, i)
+    for p, dests, mask in call:
         used += _engines(mask)
         ids = [DstId(rid=topo.addr(d)[0], pnc=topo.addr(d)[1]) for d in dests]
-        trs.append(RemoteDMATransfer(dst_ids=ids, dma_engine_mask=mask, remote_sem=rsem,
+        trs.append(RemoteDMATransfer(dst_ids=ids, dma_engine_mask=mask, remote_sem=T.sem[sem(dests[0], j, p)],
                                      srcs=[_view(T, j, p)], dsts=[_view(T, j, p) for _ in dests]))
-    g.remote_dma_fused(trs, local_sem=lsem)
+    g.remote_dma_fused(trs, local_sem=T.sem.sent)
     return used
 
 
@@ -89,25 +127,20 @@ def rank_program(g, core, T, topo):
     S = T.sem
     cores = list(T.cores)
     rank = T.rank_of(core)
-    plans = [_plan(T, topo, j) for j in range(N)]
+    jobs, land, when, sem = _plan(T, topo)
+    mine = jobs.get(core, [])
 
     if rank is None:
-        for j in range(N):
-            calls, jobs, near, far = plans[j]
-            if core not in jobs:
-                continue
-            p, dests = jobs[core]
-            got = sum(_engines(_share(topo.mask(cores[j], core), k, i))
-                      for call in calls for (_, hs, k, i) in call if core in hs)
-            g.wait_ge(S.got, got)
-            sent = 0
-            for d in dests:
-                sent += _send(g, T, topo, core, j, [(p, [d], 1, 0)], S["arr%d" % j], S.sent)
+        sent = 0
+        for (_, j, p, calls) in mine:
+            g.wait_ge(S["arr%d" % j], land[(core, "arr%d" % j)])
+            for call in calls:
+                sent += _send(g, T, topo, j, call, sem)
+        if mine:
             g.wait_ge(S.sent, sent)
         return
 
     o = NC * rank
-    calls, jobs, near, far = plans[rank]
 
     for k in range(NP):
         q = g.sync if k % 2 == 0 else g.scalar
@@ -122,23 +155,22 @@ def rank_program(g, core, T, topo):
     g.vector.quantize_mx(T.wc[:], T.ws[:], T.wb[:]).then_inc(S.qw, 1)
 
     sent = 0
-    for call in calls:
-        for p, _, _, _ in call:
-            if p < NP:
-                g.wait_ge(S["q%d" % p], 1)
-        sent += _send(g, T, topo, core, rank, call, S.got, S.sent)
-    p, dests = jobs[core]
-    sent += _send(g, T, topo, core, rank, [(p, dests, 1, 0)], S["arr%d" % rank], S.sent)
+    for (_, j, p, calls) in mine:
+        if j != rank:
+            g.wait_ge(S["rel%d" % j], land[(core, "rel%d" % j)])
+        for call in calls:
+            if j == rank:
+                for (pp, _, _) in call:
+                    if pp < NP:
+                        g.wait_ge(S["q%d" % pp], 1)
+            sent += _send(g, T, topo, j, call, sem)
 
-    def slot(j):
-        _, _, nr, fr = plans[j]
-        return (nr.index(core), 0) if core in nr else (fr.index(core), 1)
+    def arrived(j):
+        for name in ("arr%d" % j, "rel%d" % j):
+            if (core, name) in land:
+                g.tensor.wait_ge(S[name], land[(core, name)])
 
-    def expect(j):
-        _, jb, _, _ = plans[j]
-        return sum(_engines(topo.mask(c, core)) for c, (p_, ds) in jb.items() if core in ds)
-
-    order = [rank] + sorted([j for j in range(N) if j != rank], key=slot)
+    order = [rank] + sorted([j for j in range(N) if j != rank], key=lambda j: when[(core, j)])
     g.tensor.wait_ge(S.qw, 1)
     for k in range(NP):
         g.tensor.wait_ge(S["q%d" % k], 1)
@@ -146,7 +178,7 @@ def rank_program(g, core, T, topo):
     for i, j in enumerate(order[:-1]):
         a, b = NC * j, NC * j + NC
         if j != rank:
-            g.tensor.wait_ge(S["arr%d" % j], expect(j))
+            arrived(j)
         g.tensor.matmul_mx(T.ps[:, a:b], T.wc[:], T.ws[:], T.xc[:, a:b], T.xs[:, a:b], True, True).then_inc(S["mm%d" % j], 1)
         if i % 2 == 0:
             g.vector.wait_ge(S["mm%d" % j], 1)
@@ -163,7 +195,7 @@ def rank_program(g, core, T, topo):
 
     j = order[-1]
     a, h, b = NC * j, NC * j + NC // 2, NC * j + NC
-    g.tensor.wait_ge(S["arr%d" % j], expect(j))
+    arrived(j)
     g.tensor.matmul_mx(T.ps[:, a:h], T.wc[:], T.ws[:], T.xc[:, a:h], T.xs[:, a:h], True, True).then_inc(S["mm%d" % j], 1)
     g.tensor.wait_ge(S["ev%d" % rank], 1)
     g.tensor.matmul_mx(T.ps[:, o:o + NC // 2], T.wc[:], T.ws[:], T.xc[:, h:b], T.xs[:, h:b], True, True).then_inc(S.mmx, 1)

from concourse.bass import DstId, RemoteDMATransfer
from concourse.mybir import dt, ActivationFunctionType

N = 8
NC = 512
NSIM = 64
CUT = [0, 192, 384, 512]
NP = len(CUT) - 1

SCRATCH = {
    "xb": ("sbuf", [128, 4 * NC], "bfloat16"),
    "wb": ("sbuf", [128, 512], "bfloat16"),
    "wc": ("sbuf", [128, 128], "float8_e4m3fn_x4"),
    "ws": ("sbuf", [128, 128], "uint8"),
    "xc": ("sbuf", [128, N * NC], "float8_e4m3fn_x4"),
    "xs": ("sbuf", [128, N * NC], "uint8"),
    "yb": ("sbuf", [128, N * NC], "float32"),
    "ps": ("psum", [128, N * NC], "float32"),
}
SEMAPHORES = (["lw", "qw", "sent", "sts", "sta", "mmx", "evx"]
              + ["lx%d" % k for k in range(NP)] + ["q%d" % k for k in range(NP)]
              + ["arr%d" % j for j in range(N)] + ["rel%d" % j for j in range(N)]
              + ["mm%d" % j for j in range(N)] + ["ev%d" % j for j in range(N)])


def _engines(mask):
    return sum((mask >> e) & 1 for e in range(16))


def _share(mask, k, i):
    bits = [e for e in range(16) if (mask >> e) & 1]
    n = len(bits) // k
    return sum(1 << e for e in bits[i * n:(i + 1) * n])


def _plan(T, topo):
    cores = list(T.cores)
    near, mate, PS, MS = [], [], [], []
    for j, R in enumerate(cores):
        ch = topo.chip(R)
        plane = [k for k, c in enumerate(cores) if c == R or topo.same_plane(ch, topo.chip(c))]
        i = plane.index(j)
        near.append([plane[(i + s) % len(plane)] for s in range(1, len(plane))])
        mate.append([k for k, c in enumerate(cores) if topo.mates(ch, topo.chip(c))][0])
    for j, R in enumerate(cores):
        mine = [c for c in range(NSIM) if topo.chip(c) == topo.chip(R)]
        own = [c for c in mine if topo.may_write(c, cores[mate[j]])]
        rest = [c for c in mine if c not in own]
        for grp, out in ((own, MS), (rest, PS)):
            away = [c for c in grp if c != R and topo.die(c) != topo.die(R)]
            home = [c for c in grp if c != R and topo.die(c) == topo.die(R)]
            if R in grp:
                out.append(away[:1] + home + away[1:] + [R])
            else:
                out.append(away[1:] + home + away[:1])

    jobs = {}
    when = {}

    def job(core, turn, j, p, calls):
        jobs.setdefault(core, []).append((turn, j, p, calls))

    def one(src, p, d):
        return [(p, [d], topo.mask(src, d))]

    for j, R in enumerate(cores):
        c1, c2, c3 = near[j]
        who = [[c for c in (PS[j][p], MS[j][p]) if c != R] for p in range(NP + 1)]
        full = topo.mask(R, who[0][0])
        hand = [[(p, who[p], full)] for p in range(NP - 1)]
        hand.append([(NP - 1, who[NP - 1], _share(full, 2, 0)), (NP, who[NP], _share(full, 2, 1))])
        job(R, -1, j, None, hand)
        for p in range(NP + 1):
            a, b = PS[j][p], MS[j][p]
            job(a, 0, j, p, [one(a, p, MS[c1][p]), one(a, p, MS[c2][p]), one(a, p, cores[c3])])
            job(b, 0, j, p, [one(b, p, cores[mate[c3]]), one(b, p, cores[mate[j]])])
            for turn, c in ((1, c1), (2, c2)):
                q = MS[c][p]
                off = topo.mask(q, cores[mate[c]])
                call = [(p, [cores[mate[c]]], off)]
                if q != cores[c]:
                    call.insert(0, (p, [cores[c]], topo.mask(q, cores[c]) & ~off))
                job(q, turn, j, p, [call])
        when[(cores[mate[c3]], j)] = (0, 0)
        when[(cores[mate[j]], j)] = (0, 1)
        when[(cores[c3], j)] = (0, 2)
        for turn, c in ((1, c1), (2, c2)):
            when[(cores[c], j)] = (turn, 0)
            when[(cores[mate[c]], j)] = (turn, 1)

    passes = set((core, j, p) for core, js in jobs.items() for (_, j, p, _) in js if p is not None)

    def sem(d, j, p):
        return ("rel%d" if (d in cores and (d, j, p) in passes) else "arr%d") % j

    land = {}
    for core, js in jobs.items():
        js.sort(key=lambda t: t[0])
        for (_, j, _, calls) in js:
            for call in calls:
                for (p, dests, mask) in call:
                    for d in dests:
                        k = (d, sem(d, j, p))
                        land[k] = land.get(k, 0) + _engines(mask)
    return jobs, land, when, sem


def _view(T, j, p):
    if p < NP:
        return T.xc[:, NC * j + CUT[p]:NC * j + CUT[p + 1]].bitcast(dt.uint8)
    return T.xs[:, NC * j:NC * j + NC]


def _send(g, T, topo, j, call, sem):
    trs = []
    used = 0
    for p, dests, mask in call:
        used += _engines(mask)
        ids = [DstId(rid=topo.addr(d)[0], pnc=topo.addr(d)[1]) for d in dests]
        trs.append(RemoteDMATransfer(dst_ids=ids, dma_engine_mask=mask, remote_sem=T.sem[sem(dests[0], j, p)],
                                     srcs=[_view(T, j, p)], dsts=[_view(T, j, p) for _ in dests]))
    g.remote_dma_fused(trs, local_sem=T.sem.sent)
    return used


def rank_program(g, core, T, topo):
    S = T.sem
    cores = list(T.cores)
    rank = T.rank_of(core)
    jobs, land, when, sem = _plan(T, topo)
    mine = jobs.get(core, [])

    if rank is None:
        sent = 0
        for (_, j, p, calls) in mine:
            g.wait_ge(S["arr%d" % j], land[(core, "arr%d" % j)])
            for call in calls:
                sent += _send(g, T, topo, j, call, sem)
        if mine:
            g.wait_ge(S.sent, sent)
        return

    o = NC * rank

    for k in range(NP):
        q = g.sync if k % 2 == 0 else g.scalar
        q.dma_start(T.xb[:, 4 * CUT[k]:4 * CUT[k + 1]], T.x[:, 4 * CUT[k]:4 * CUT[k + 1]]).then_inc(S["lx%d" % k], 16)
    g.scalar.dma_start(T.wb[:], T.w[:]).then_inc(S.lw, 16)

    for k in range(NP):
        g.vector.wait_ge(S["lx%d" % k], 16)
        g.vector.quantize_mx(T.xc[:, o + CUT[k]:o + CUT[k + 1]], T.xs[:, o + CUT[k]:o + CUT[k + 1]],
                             T.xb[:, 4 * CUT[k]:4 * CUT[k + 1]]).then_inc(S["q%d" % k], 1)
    g.vector.wait_ge(S.lw, 16)
    g.vector.quantize_mx(T.wc[:], T.ws[:], T.wb[:]).then_inc(S.qw, 1)

    sent = 0
    for (_, j, p, calls) in mine:
        if j != rank:
            g.wait_ge(S["rel%d" % j], land[(core, "rel%d" % j)])
        for call in calls:
            if j == rank:
                for (pp, _, _) in call:
                    if pp < NP:
                        g.wait_ge(S["q%d" % pp], 1)
            sent += _send(g, T, topo, j, call, sem)

    def arrived(j):
        for name in ("arr%d" % j, "rel%d" % j):
            if (core, name) in land:
                g.tensor.wait_ge(S[name], land[(core, name)])

    order = [rank] + sorted([j for j in range(N) if j != rank], key=lambda j: when[(core, j)])
    g.tensor.wait_ge(S.qw, 1)
    for k in range(NP):
        g.tensor.wait_ge(S["q%d" % k], 1)
    n_sync = n_act = 0
    for i, j in enumerate(order[:-1]):
        a, b = NC * j, NC * j + NC
        if j != rank:
            arrived(j)
        g.tensor.matmul_mx(T.ps[:, a:b], T.wc[:], T.ws[:], T.xc[:, a:b], T.xs[:, a:b], True, True).then_inc(S["mm%d" % j], 1)
        if i % 2 == 0:
            g.vector.wait_ge(S["mm%d" % j], 1)
            g.vector.tensor_copy(T.yb[:, a:b], T.ps[:, a:b]).then_inc(S["ev%d" % j], 1)
            g.sync.wait_ge(S["ev%d" % j], 1)
            g.sync.dma_start(T.y[:, a:b], T.yb[:, a:b]).then_inc(S.sts, 16)
            n_sync += 1
        else:
            g.scalar.wait_ge(S["mm%d" % j], 1)
            g.scalar.activation(T.yb[:, a:b], T.ps[:, a:b], ActivationFunctionType.Copy).then_inc(S["ev%d" % j], 1)
            g.scalar.wait_ge(S["ev%d" % j], 1)
            g.scalar.dma_start(T.y[:, a:b], T.yb[:, a:b]).then_inc(S.sta, 16)
            n_act += 1

    j = order[-1]
    a, h, b = NC * j, NC * j + NC // 2, NC * j + NC
    arrived(j)
    g.tensor.matmul_mx(T.ps[:, a:h], T.wc[:], T.ws[:], T.xc[:, a:h], T.xs[:, a:h], True, True).then_inc(S["mm%d" % j], 1)
    g.tensor.wait_ge(S["ev%d" % rank], 1)
    g.tensor.matmul_mx(T.ps[:, o:o + NC // 2], T.wc[:], T.ws[:], T.xc[:, h:b], T.xs[:, h:b], True, True).then_inc(S.mmx, 1)
    g.vector.wait_ge(S["mm%d" % j], 1)
    g.vector.tensor_copy(T.yb[:, a:h], T.ps[:, a:h]).then_inc(S["ev%d" % j], 1)
    g.sync.wait_ge(S["ev%d" % j], 1)
    g.sync.dma_start(T.y[:, a:h], T.yb[:, a:h]).then_inc(S.sts, 16)
    g.scalar.wait_ge(S.mmx, 1)
    g.scalar.activation(T.yb[:, h:b], T.ps[:, o:o + NC // 2], ActivationFunctionType.Copy).then_inc(S.evx, 1)
    g.scalar.wait_ge(S.evx, 1)
    g.scalar.dma_start(T.y[:, h:b], T.yb[:, h:b]).then_inc(S.sta, 16)

    g.sync.wait_ge(S.sts, 16 * (n_sync + 1))
    g.scalar.wait_ge(S.sta, 16 * (n_act + 1))
    g.wait_ge(S.sent, sent)
